import numpy as np
import ml_dtypes


def mxq(x, axis, fmt="e4m3"):
    dtype, down = {"e4m3": (ml_dtypes.float8_e4m3fn, 7), "e5m2": (ml_dtypes.float8_e5m2, 14)}[fmt]
    v = np.moveaxis(np.asarray(x, np.float32).astype(ml_dtypes.bfloat16).astype(np.float64), axis, -1)
    blocks = v.reshape(v.shape[:-1] + (-1, 32))
    amax = np.abs(blocks).max(-1, keepdims=True)
    byte = np.maximum(np.where(amax > 0, np.frexp(amax)[1] - 1 + 127, 0) - down, 1)
    scale = np.exp2(byte - 127.0)
    codes = (blocks / scale).astype(np.float32).astype(dtype).astype(np.float64)
    return np.moveaxis((codes * scale).reshape(v.shape), -1, axis)


WIDE = False


def mx_kscale(k):
    if not WIDE:
        return np.ones(k)
    levels = np.array([10, -10, 5, -5, 0])
    if k % 512:
        return np.exp2(np.random.permutation(np.resize(levels, k // 32))).repeat(32)
    a = np.empty((k // 512, 16))
    for p in range(k // 512):
        a[p, :8] = np.random.permutation(np.resize(levels, 8))
        for g in range(8):
            far = levels[np.abs(levels - a[p, g]) >= 10]
            a[p, g + 8] = far[np.random.randint(len(far))]
    return np.exp2(a.ravel()).repeat(32)


def f64(x):
    return np.asarray(x).astype(np.float64)


def striped(idx):
    return np.tile(idx.reshape(-1, 16).T, (8, 1)).astype(np.uint16)


def unstriped(offs):
    return offs[:16].T.reshape(-1).astype(np.int64)


def pack_weight(w):
    k, n = w.shape
    w = f64(np.asarray(w, np.float32).astype(ml_dtypes.bfloat16)).reshape(k // 32, 32, n)
    amax = np.abs(w).max(1)
    byte = np.clip(np.where(amax > 0, np.frexp(amax)[1] - 1 + 127 - 7, 1), 1, 254)
    scaled = (w * np.exp2(127.0 - byte)[:, None, :]).reshape(k, n).astype(np.float32)
    words = np.ascontiguousarray(scaled.reshape(k // 512, 128, 4, n).transpose(0, 1, 3, 2)).astype(ml_dtypes.float8_e4m3fn).view(np.uint8)
    return words, np.ascontiguousarray(byte.astype(np.uint8).reshape(k // 512, 16, n))


def unpack_weight(words, scales):
    g, p, n, _ = words.shape
    vals = np.ascontiguousarray(words).view(ml_dtypes.float8_e4m3fn).astype(np.float64) * np.repeat(np.exp2(scales.astype(np.float64) - 127.0), 8, axis=1)[..., None]
    return vals.transpose(0, 1, 3, 2).reshape(g * 512, n)


def sigmoid(v):
    return 1.0 / (1.0 + np.exp(-np.maximum(v, -700.0)))


K, T, S, D, N, H, V, U = 512, 2048, 1024, 4, 128, 512, 256, 512


def setup_inputs():
    n = np.random.standard_normal
    s = mx_kscale(K)[:, None]
    u = mx_kscale(H)
    packed_xT = pack_weight(n((K, T)) * s)
    return {
        "x_words": packed_xT[0],
        "x_scales": packed_xT[1],
        "w1": (n((K, H)) / np.sqrt(K) / s).astype(np.float32),
        "thr": (np.random.uniform(-0.3, 0.8, (H, U))).astype(np.float32),
        "mk": (n((H, U))).astype(np.float32),
        "unit": (np.random.uniform(0.6, 1.4, (H, 1)) * u[:, None]).astype(np.float32),
        "w2": (n((H, N)) / np.sqrt(H) / u[:, None]).astype(np.float32),
        "offs": striped(np.random.permutation(T)[:S]),
        "slot": striped(np.random.permutation(np.concatenate([np.arange(V), np.random.randint(0, V, U - V)]))),
    }


def reference(x_words, x_scales, w1, thr, mk, unit, w2, offs, slot):
    xq = unpack_weight(x_words, x_scales)[:, unstriped(offs)]
    y = mxq(f64(w1), 0, "e4m3").T @ xq
    prtop = y.reshape(len(y), -1, D).max(axis=2)
    prexp = np.exp(y - np.repeat(prtop, D, axis=1))
    prsum = prexp.reshape(len(prexp), -1, D).sum(axis=2)
    pr = prexp / np.repeat(prsum, D, axis=1)
    py = pr * y
    ev = py.reshape(len(py), -1, D).sum(axis=2)
    cs = ev[:, unstriped(slot)]
    kp = sigmoid(2.0 * (cs - f64(thr)))
    best = y.reshape(len(y), -1, D).max(axis=2)
    ms = best[:, unstriped(slot)]
    hid = f64(unit) * (kp * ms + (-1.0 * kp + 1.0) * f64(mk))
    return mxq(f64(w2), 0, "e4m3").T @ mxq(hid, 0, "e4m3")

@@ -1,0 +1,208 @@
+from contextlib import ExitStack
+
+import concourse.mybir as mybir
+from concourse.masks import make_identity
+
+K, T, S, D, N, H, V, U = 512, 2048, 1024, 4, 128, 512, 256, 512
+FLOPS = 2 * K * H * S + 2 * H * N * U
+
+F32 = mybir.dt.float32
+BF16 = mybir.dt.bfloat16
+I32 = mybir.dt.int32
+U32 = mybir.dt.uint32
+U16 = mybir.dt.uint16
+U8 = mybir.dt.uint8
+FP8X4 = mybir.dt.float8_e4m3fn_x4
+ALU = mybir.AluOpType
+ACT = mybir.ActivationFunctionType
+AX = mybir.AxisListType
+
+P = 128
+PACK = 4
+HALF = 512
+GROUPS = HALF // D
+WINDOW = U + 16
+GUESS_RATE = 0.9625
+GUESS_FLOOR = 0.107
+
+
+def tile_picked_ymaskd_mix_p_kernel(
+    tc, x_words, x_scales, w1, thr, mk, unit, w2, offs, slot, out
+):
+    nc = tc.nc
+    with ExitStack() as ctx:
+        keep = ctx.enter_context(tc.tile_pool(name="keep", bufs=1))
+        ring = ctx.enter_context(tc.tile_pool(name="ring", bufs=3))
+        psum = ctx.enter_context(tc.psum_pool(name="psum", bufs=1))
+
+        offs_sb = keep.tile([P, S // 16], U16, name="offs_sb")
+        slot_sb = keep.tile([P, U // 16], U16, name="slot_sb")
+        xs = keep.tile([P, T], U8, name="xs", align_bytes=64)
+        nc.vector.memset(xs[:].bitcast(I32), 0)
+        nc.sync.dma_start(offs_sb[:], offs)
+        w1v = w1.rearrange("(p j) c -> p j c", j=PACK)
+        w1_raw = []
+        for s in range(2):
+            raw = keep.tile([P, PACK, H // 2], F32, name="w1_raw%d" % s)
+            nc.sync.dma_start(out=raw[:], in_=w1v[:, :, s * (H // 2) : (s + 1) * (H // 2)])
+            w1_raw.append(raw)
+        xw = keep.tile([P, T], I32, name="xw", align_bytes=64)
+        nc.sync.dma_start(out=xw[:], in_=x_words[0].rearrange("p n t -> p (n t)").bitcast(I32))
+        for q in range(4):
+            nc.scalar.dma_start(
+                out=xs[32 * q : 32 * q + 4, :].bitcast(I32), in_=x_scales[0, 4 * q : 4 * q + 4, :].bitcast(I32)
+            )
+        unit_sb = keep.tile([P, PACK], F32, name="unit_sb")
+        nc.sync.dma_start(out=unit_sb[:], in_=unit.rearrange("(p t) o -> p (t o)", t=PACK))
+        nc.sync.dma_start(slot_sb[:], slot)
+        mk_sb = keep.tile([P, PACK, U], F32, name="mk_sb")
+        nc.sync.dma_start(out=mk_sb[:], in_=mk.rearrange("(p t) r -> p t r", t=PACK))
+        thr_sb = keep.tile([P, PACK, U], F32, name="thr_sb")
+        nc.sync.dma_start(out=thr_sb[:], in_=thr.rearrange("(p t) r -> p t r", t=PACK))
+        w2_raw = keep.tile([P, PACK, N], F32, name="w2_raw")
+        nc.sync.dma_start(out=w2_raw[:], in_=w2.rearrange("(p j) n -> p j n", j=PACK))
+
+        ident = keep.tile([P, P], F32, name="ident")
+        make_identity(nc, ident[:])
+        best_win, ev_win = [], []
+        for t in range(PACK):
+            bw = keep.tile([P, WINDOW], F32, name="best_win%d" % t)
+            ew = keep.tile([P, WINDOW], F32, name="ev_win%d" % t)
+            nc.gpsimd.memset(bw[:, V:], 0.0)
+            nc.gpsimd.memset(ew[:, V:], 0.0)
+            best_win.append(bw)
+            ev_win.append(ew)
+
+        w1_bf = keep.tile([P, PACK, P, PACK], BF16, name="w1_bf", align_bytes=64)
+        for s in range(2):
+            dst = w1_bf[:, :, s * 64 : (s + 1) * 64, :].rearrange("p t m j -> p m j t")
+            src = w1_raw[s][:].rearrange("p j (m t) -> p m j t", t=PACK)
+            if s == 0:
+                nc.scalar.activation(dst, src, ACT.Copy)
+            else:
+                nc.vector.tensor_copy(dst, src)
+        w1_codes = keep.tile([P, PACK, P], U32, name="w1_codes", align_bytes=64)
+        w1_sc = keep.tile([P, PACK, P], U8, name="w1_sc", align_bytes=64)
+        for t in range(PACK):
+            nc.vector.quantize_mx(
+                out=w1_codes[:, t, :].bitcast(FP8X4),
+                scales=w1_sc[:, t, :],
+                in_=w1_bf[:, t, :, :].rearrange("p m j -> p (m j)"),
+            )
+
+        x_codes, x_sc = [], []
+        for h in range(2):
+            xc = keep.tile([P, HALF], U32, name="x_codes%d" % h, align_bytes=64)
+            xb = keep.tile([P, HALF], U8, name="x_sc%d" % h, align_bytes=64)
+            part = offs_sb[:, h * (HALF // 16) : (h + 1) * (HALF // 16)]
+            nc.vector.tensor_copy(xc[:], xw[:].bitcast(U32).indirect(part))
+            nc.vector.tensor_copy(xb[:], xs[:].indirect(part))
+            x_codes.append(xc)
+            x_sc.append(xb)
+
+        half_unit = keep.tile([P, PACK], F32, name="half_unit")
+        nc.gpsimd.tensor_scalar(half_unit[:], unit_sb[:], 0.5, 0.0, ALU.mult, ALU.add)
+        mask_u = keep.tile([P, PACK, U], F32, name="mask_u")
+        mask_hu = keep.tile([P, PACK, U], F32, name="mask_hu")
+        for t in range(PACK):
+            nc.gpsimd.tensor_scalar(mask_hu[:, t, :], mk_sb[:, t, :], unit_sb[:, t : t + 1], 0.5, ALU.mult, ALU.mult)
+        for t in range(PACK):
+            nc.gpsimd.tensor_scalar(mask_u[:, t, :], mk_sb[:, t, :], unit_sb[:, t : t + 1], 0.0, ALU.mult, ALU.add)
+
+        kept = keep.tile([P, PACK, U], F32, name="kept")
+        for t in range(PACK):
+            ssum = psum.tile([P, V], F32, name="ssum", bufs=1)
+            nsum = psum.tile([P, V], F32, name="nsum", bufs=1)
+            for h in range(2):
+                cols = slice(h * GROUPS, (h + 1) * GROUPS)
+                y = psum.tile([P, HALF], F32, name="y", bufs=4)
+                nc.tensor.matmul_mx(
+                    out=y[:],
+                    lhsT=w1_codes[:, t, :].bitcast(FP8X4),
+                    lhsT_scale=w1_sc[:, t, :],
+                    rhs=x_codes[h][:].bitcast(FP8X4),
+                    rhs_scale=x_sc[h][:],
+                    start=True,
+                    stop=True,
+                )
+                top = best_win[t][:, cols]
+                nc.vector.tensor_reduce(top, y[:].rearrange("p (v d) -> p v d", d=D), AX.X, ALU.max)
+                y_planes = y[:].rearrange("p (v d) -> p d v", d=D)
+                z = ring.tile([P, D, GROUPS], F32, name="z")
+                nc.vector.tensor_tensor(z[:], y_planes, top.unsqueeze(1).to_broadcast([P, D, GROUPS]), ALU.subtract)
+                e = ring.tile([P, D, GROUPS], F32, name="e")
+                nc.scalar.activation(e[:], z[:], ACT.Exp)
+                ey = ring.tile([P, D, GROUPS], F32, name="ey")
+                nc.vector.tensor_tensor(ey[:], y_planes, e[:], ALU.mult)
+                for d in range(D):
+                    nc.tensor.matmul(ssum[:, cols], e[:, d, :], ident[:], start=(d == 0), stop=(d == D - 1), is_transpose=True)
+                for d in range(D):
+                    nc.tensor.matmul(nsum[:, cols], ey[:, d, :], ident[:], start=(d == 0), stop=(d == D - 1), is_transpose=True)
+
+            ms = ring.tile([P, U], F32, name="ms")
+            nc.scalar.activation(ms[:], best_win[t][:].indirect(slot_sb[:]), ACT.Copy)
+            gap = ring.tile([P, U], F32, name="gap")
+            nc.vector.scalar_tensor_tensor(gap[:], ms[:], half_unit[:, t : t + 1], mask_hu[:, t, :], ALU.mult, ALU.subtract)
+
+            guess = ring.tile([P, V], F32, name="guess")
+            nc.scalar.activation(guess[:], ssum[:], ACT.Exp, scale=-GUESS_RATE)
+            half_t = ring.tile([P, V], F32, name="half_t")
+            nc.vector.scalar_tensor_tensor(half_t[:], guess[:], GUESS_FLOOR, ssum[:], ALU.add, ALU.mult)
+            q1 = ring.tile([P, V], F32, name="q1")
+            nc.vector.scalar_tensor_tensor(q1[:], guess[:], GUESS_FLOOR, nsum[:], ALU.add, ALU.mult)
+            eps2 = ring.tile([P, V], F32, name="eps2")
+            nc.scalar.activation(eps2[:], half_t[:], ACT.Square, bias=-1.0, scale=2.0)
+            series = ring.tile([P, V], F32, name="series")
+            nc.scalar.activation(series[:], eps2[:], ACT.Square, bias=0.5)
+            q2 = ring.tile([P, V], F32, name="q2")
+            nc.vector.scalar_tensor_tensor(q2[:], half_t[:], 1.0, q1[:], ALU.subtract, ALU.mult)
+            q3 = ring.tile([P, V], F32, name="q3")
+            nc.vector.scalar_tensor_tensor(q3[:], series[:], 0.75, q2[:], ALU.add, ALU.mult)
+            back = psum.tile([P, V], F32, name="back", bufs=1)
+            for h in range(2):
+                cols = slice(h * GROUPS, (h + 1) * GROUPS)
+                nc.tensor.transpose(back[:, cols], q3[:, cols], ident[:])
+            nc.scalar.activation(ev_win[t][:, :V], back[:], ACT.Copy, scale=-4.0)
+
+            cs = ring.tile([P, U], F32, name="cs")
+            nc.scalar.activation(cs[:], ev_win[t][:].indirect(slot_sb[:]), ACT.Copy)
+            margin = ring.tile([P, U], F32, name="margin")
+            nc.vector.tensor_tensor(margin[:], cs[:], thr_sb[:, t, :], ALU.subtract)
+            th = ring.tile([P, U], F32, name="th")
+            nc.scalar.activation(th[:], margin[:], ACT.Tanh)
+            nc.vector.scalar_tensor_tensor(kept[:, t, :], th[:], 1.0, gap[:], ALU.add, ALU.mult)
+
+        w2_bf = keep.tile([P, N, PACK], BF16, name="w2_bf", align_bytes=64)
+        nc.scalar.activation(
+            w2_bf[:].rearrange("p (c i) j -> p c j i", i=4), w2_raw[:].rearrange("p j (c i) -> p c j i", i=4), ACT.Copy
+        )
+        w2_codes = keep.tile([P, N], U32, name="w2_codes", align_bytes=64)
+        w2_sc = keep.tile([P, N], U8, name="w2_sc", align_bytes=64)
+        nc.vector.quantize_mx(out=w2_codes[:].bitcast(FP8X4), scales=w2_sc[:], in_=w2_bf[:].rearrange("p n j -> p (n j)"))
+
+        RW = U // 2
+        for g in range(2):
+            cols = slice(g * RW, (g + 1) * RW)
+            hid = keep.tile([P, RW, PACK], BF16, name="hid%d" % g, align_bytes=64)
+            nc.vector.tensor_tensor(
+                hid[:].rearrange("p (c i) t -> p c t i", i=4),
+                kept[:, :, cols].rearrange("p t (c i) -> p c t i", i=4),
+                mask_u[:, :, cols].rearrange("p t (c i) -> p c t i", i=4),
+                ALU.add,
+            )
+            h_codes = keep.tile([P, RW], U32, name="h_codes%d" % g, align_bytes=64)
+            h_sc = keep.tile([P, RW], U8, name="h_sc%d" % g, align_bytes=64)
+            nc.vector.quantize_mx(out=h_codes[:].bitcast(FP8X4), scales=h_sc[:], in_=hid[:].rearrange("p r t -> p (r t)"))
+            acc = psum.tile([P, HALF], F32, name="y", bufs=4)
+            nc.tensor.matmul_mx(
+                out=acc[:, :RW],
+                lhsT=w2_codes[:].bitcast(FP8X4),
+                lhsT_scale=w2_sc[:],
+                rhs=h_codes[:].bitcast(FP8X4),
+                rhs_scale=h_sc[:],
+                start=True,
+                stop=True,
+            )
+            res = keep.tile([P, RW], F32, name="res%d" % g)
+            nc.scalar.activation(res[:], acc[:, :RW], ACT.Copy)
+            nc.sync.dma_start(out=out[:, cols], in_=res[:])

@@ -32,7 +32,7 @@ def tile_picked_ymaskd_mix_p_kernel(
     nc = tc.nc
     with ExitStack() as ctx:
         keep = ctx.enter_context(tc.tile_pool(name="keep", bufs=1))
-        ring = ctx.enter_context(tc.tile_pool(name="ring", bufs=3))
+        ring = ctx.enter_context(tc.tile_pool(name="ring", bufs=4))
         psum = ctx.enter_context(tc.psum_pool(name="psum", bufs=1))
 
         offs_sb = keep.tile([P, S // 16], U16, name="offs_sb")
@@ -40,27 +40,21 @@ def tile_picked_ymaskd_mix_p_kernel(
         xs = keep.tile([P, T], U8, name="xs", align_bytes=64)
         nc.vector.memset(xs[:].bitcast(I32), 0)
         nc.sync.dma_start(offs_sb[:], offs)
+        xw = keep.tile([P, T], I32, name="xw", align_bytes=64)
+        nc.sync.dma_start(out=xw[:], in_=x_words[0].rearrange("p n t -> p (n t)").bitcast(I32))
         w1v = w1.rearrange("(p j) c -> p j c", j=PACK)
         w1_raw = []
         for s in range(2):
-            raw = keep.tile([P, PACK, H // 2], F32, name="w1_raw%d" % s)
+            raw = keep.tile([P, PACK, H // 2], F32, name="w1_raw%d" % s, tag="stage%d" % s)
             nc.sync.dma_start(out=raw[:], in_=w1v[:, :, s * (H // 2) : (s + 1) * (H // 2)])
             w1_raw.append(raw)
-        xw = keep.tile([P, T], I32, name="xw", align_bytes=64)
-        nc.sync.dma_start(out=xw[:], in_=x_words[0].rearrange("p n t -> p (n t)").bitcast(I32))
         for q in range(4):
             nc.scalar.dma_start(
                 out=xs[32 * q : 32 * q + 4, :].bitcast(I32), in_=x_scales[0, 4 * q : 4 * q + 4, :].bitcast(I32)
             )
-        unit_sb = keep.tile([P, PACK], F32, name="unit_sb")
-        nc.sync.dma_start(out=unit_sb[:], in_=unit.rearrange("(p t) o -> p (t o)", t=PACK))
         nc.sync.dma_start(slot_sb[:], slot)
-        mk_sb = keep.tile([P, PACK, U], F32, name="mk_sb")
-        nc.sync.dma_start(out=mk_sb[:], in_=mk.rearrange("(p t) r -> p t r", t=PACK))
-        thr_sb = keep.tile([P, PACK, U], F32, name="thr_sb")
-        nc.sync.dma_start(out=thr_sb[:], in_=thr.rearrange("(p t) r -> p t r", t=PACK))
-        w2_raw = keep.tile([P, PACK, N], F32, name="w2_raw")
-        nc.sync.dma_start(out=w2_raw[:], in_=w2.rearrange("(p j) n -> p j n", j=PACK))
+        unit_sb = keep.tile([P, PACK], F32, name="unit_sb")
+        nc.gpsimd.dma_start(out=unit_sb[:], in_=unit.rearrange("(p t) o -> p (t o)", t=PACK))
 
         ident = keep.tile([P, P], F32, name="ident")
         make_identity(nc, ident[:])
@@ -73,14 +67,18 @@ def tile_picked_ymaskd_mix_p_kernel(
             best_win.append(bw)
             ev_win.append(ew)
 
-        w1_bf = keep.tile([P, PACK, P, PACK], BF16, name="w1_bf", align_bytes=64)
+        x_codes = [keep.tile([P, HALF], U32, name="x_codes%d" % h, align_bytes=64) for h in range(2)]
+        x_sc = [keep.tile([P, HALF], U8, name="x_sc%d" % h, align_bytes=64) for h in range(2)]
+        parts = [offs_sb[:, h * (HALF // 16) : (h + 1) * (HALF // 16)] for h in range(2)]
+        for h in range(2):
+            nc.vector.tensor_copy(x_codes[h][:], xw[:].bitcast(U32).indirect(parts[h]))
+        nc.vector.tensor_copy(x_sc[0][:], xs[:].indirect(parts[0]))
+
+        w1_bf = keep.tile([P, PACK, P, PACK], BF16, name="w1_bf", tag="stage2", align_bytes=64)
         for s in range(2):
             dst = w1_bf[:, :, s * 64 : (s + 1) * 64, :].rearrange("p t m j -> p m j t")
             src = w1_raw[s][:].rearrange("p j (m t) -> p m j t", t=PACK)
-            if s == 0:
-                nc.scalar.activation(dst, src, ACT.Copy)
-            else:
-                nc.vector.tensor_copy(dst, src)
+            nc.scalar.activation(dst, src, ACT.Copy)
         w1_codes = keep.tile([P, PACK, P], U32, name="w1_codes", align_bytes=64)
         w1_sc = keep.tile([P, PACK, P], U8, name="w1_sc", align_bytes=64)
         for t in range(PACK):
@@ -89,16 +87,14 @@ def tile_picked_ymaskd_mix_p_kernel(
                 scales=w1_sc[:, t, :],
                 in_=w1_bf[:, t, :, :].rearrange("p m j -> p (m j)"),
             )
+        nc.vector.tensor_copy(x_sc[1][:], xs[:].indirect(parts[1]))
 
-        x_codes, x_sc = [], []
-        for h in range(2):
-            xc = keep.tile([P, HALF], U32, name="x_codes%d" % h, align_bytes=64)
-            xb = keep.tile([P, HALF], U8, name="x_sc%d" % h, align_bytes=64)
-            part = offs_sb[:, h * (HALF // 16) : (h + 1) * (HALF // 16)]
-            nc.vector.tensor_copy(xc[:], xw[:].bitcast(U32).indirect(part))
-            nc.vector.tensor_copy(xb[:], xs[:].indirect(part))
-            x_codes.append(xc)
-            x_sc.append(xb)
+        mk_sb = keep.tile([P, PACK, U], F32, name="mk_sb", tag="stage0")
+        nc.sync.dma_start(out=mk_sb[:], in_=mk.rearrange("(p t) r -> p t r", t=PACK))
+        thr_sb = keep.tile([P, PACK, U], F32, name="thr_sb", tag="stage1")
+        nc.sync.dma_start(out=thr_sb[:], in_=thr.rearrange("(p t) r -> p t r", t=PACK))
+        w2_raw = keep.tile([P, PACK, N], F32, name="w2_raw", tag="stage2", align_bytes=64)
+        nc.sync.dma_start(out=w2_raw[:], in_=w2.rearrange("(p j) n -> p j n", j=PACK))
 
         half_unit = keep.tile([P, PACK], F32, name="half_unit")
         nc.gpsimd.tensor_scalar(half_unit[:], unit_sb[:], 0.5, 0.0, ALU.mult, ALU.add)
@@ -110,12 +106,14 @@ def tile_picked_ymaskd_mix_p_kernel(
             nc.gpsimd.tensor_scalar(mask_u[:, t, :], mk_sb[:, t, :], unit_sb[:, t : t + 1], 0.0, ALU.mult, ALU.add)
 
         kept = keep.tile([P, PACK, U], F32, name="kept")
-        for t in range(PACK):
-            ssum = psum.tile([P, V], F32, name="ssum", bufs=1)
-            nsum = psum.tile([P, V], F32, name="nsum", bufs=1)
+        gap = keep.tile([P, PACK, U], F32, name="gap")
+
+        def scores(t):
+            ssum = psum.tile([P, V], F32, name="ssum", bufs=2)
+            nsum = psum.tile([P, V], F32, name="nsum", bufs=2)
             for h in range(2):
                 cols = slice(h * GROUPS, (h + 1) * GROUPS)
-                y = psum.tile([P, HALF], F32, name="y", bufs=4)
+                y = psum.tile([P, HALF], F32, name="y", bufs=3)
                 nc.tensor.matmul_mx(
                     out=y[:],
                     lhsT=w1_codes[:, t, :].bitcast(FP8X4),
@@ -138,22 +136,19 @@ def tile_picked_ymaskd_mix_p_kernel(
                     nc.tensor.matmul(ssum[:, cols], e[:, d, :], ident[:], start=(d == 0), stop=(d == D - 1), is_transpose=True)
                 for d in range(D):
                     nc.tensor.matmul(nsum[:, cols], ey[:, d, :], ident[:], start=(d == 0), stop=(d == D - 1), is_transpose=True)
+            return ssum, nsum
 
-            ms = ring.tile([P, U], F32, name="ms")
-            nc.scalar.activation(ms[:], best_win[t][:].indirect(slot_sb[:]), ACT.Copy)
-            gap = ring.tile([P, U], F32, name="gap")
-            nc.vector.scalar_tensor_tensor(gap[:], ms[:], half_unit[:, t : t + 1], mask_hu[:, t, :], ALU.mult, ALU.subtract)
-
+        def divide(t, ssum, nsum):
             guess = ring.tile([P, V], F32, name="guess")
             nc.scalar.activation(guess[:], ssum[:], ACT.Exp, scale=-GUESS_RATE)
             half_t = ring.tile([P, V], F32, name="half_t")
             nc.vector.scalar_tensor_tensor(half_t[:], guess[:], GUESS_FLOOR, ssum[:], ALU.add, ALU.mult)
-            q1 = ring.tile([P, V], F32, name="q1")
-            nc.vector.scalar_tensor_tensor(q1[:], guess[:], GUESS_FLOOR, nsum[:], ALU.add, ALU.mult)
             eps2 = ring.tile([P, V], F32, name="eps2")
             nc.scalar.activation(eps2[:], half_t[:], ACT.Square, bias=-1.0, scale=2.0)
             series = ring.tile([P, V], F32, name="series")
             nc.scalar.activation(series[:], eps2[:], ACT.Square, bias=0.5)
+            q1 = ring.tile([P, V], F32, name="q1")
+            nc.vector.scalar_tensor_tensor(q1[:], guess[:], GUESS_FLOOR, nsum[:], ALU.add, ALU.mult)
             q2 = ring.tile([P, V], F32, name="q2")
             nc.vector.scalar_tensor_tensor(q2[:], half_t[:], 1.0, q1[:], ALU.subtract, ALU.mult)
             q3 = ring.tile([P, V], F32, name="q3")
@@ -164,13 +159,32 @@ def tile_picked_ymaskd_mix_p_kernel(
                 nc.tensor.transpose(back[:, cols], q3[:, cols], ident[:])
             nc.scalar.activation(ev_win[t][:, :V], back[:], ACT.Copy, scale=-4.0)
 
-            cs = ring.tile([P, U], F32, name="cs")
-            nc.scalar.activation(cs[:], ev_win[t][:].indirect(slot_sb[:]), ACT.Copy)
-            margin = ring.tile([P, U], F32, name="margin")
-            nc.vector.tensor_tensor(margin[:], cs[:], thr_sb[:, t, :], ALU.subtract)
-            th = ring.tile([P, U], F32, name="th")
+        def gaps(t):
+            ms = ring.tile([P, U], F32, name="ms")
+            nc.scalar.activation(ms[:], best_win[t][:].indirect(slot_sb[:]), ACT.Copy)
+            nc.vector.scalar_tensor_tensor(gap[:, t, :], ms[:], half_unit[:, t : t + 1], mask_hu[:, t, :], ALU.mult, ALU.subtract)
+
+        def keeps(t, r0, r1):
+            cs = ring.tile([P, r1 - r0], F32, name="cs")
+            nc.scalar.activation(cs[:], ev_win[t][:].indirect(slot_sb[:, r0 // 16 : r1 // 16]), ACT.Copy)
+            margin = ring.tile([P, r1 - r0], F32, name="margin")
+            nc.vector.tensor_tensor(margin[:], cs[:], thr_sb[:, t, r0:r1], ALU.subtract)
+            th = ring.tile([P, r1 - r0], F32, name="th")
             nc.scalar.activation(th[:], margin[:], ACT.Tanh)
-            nc.vector.scalar_tensor_tensor(kept[:, t, :], th[:], 1.0, gap[:], ALU.add, ALU.mult)
+            nc.vector.scalar_tensor_tensor(kept[:, t, r0:r1], th[:], 1.0, gap[:, t, r0:r1], ALU.add, ALU.mult)
+
+        sums = []
+        for t in range(PACK):
+            sums.append(scores(t))
+            if t > 0:
+                divide(t - 1, *sums[t - 1])
+        divide(PACK - 1, *sums[PACK - 1])
+        for t in range(PACK):
+            gaps(t)
+            if t < PACK - 1:
+                keeps(t, 0, U)
+        for g in range(2):
+            keeps(PACK - 1, g * (U // 2), (g + 1) * (U // 2))
 
         w2_bf = keep.tile([P, N, PACK], BF16, name="w2_bf", align_bytes=64)
         nc.scalar.activation(
@@ -193,7 +207,7 @@ def tile_picked_ymaskd_mix_p_kernel(
             h_codes = keep.tile([P, RW], U32, name="h_codes%d" % g, align_bytes=64)
             h_sc = keep.tile([P, RW], U8, name="h_sc%d" % g, align_bytes=64)
             nc.vector.quantize_mx(out=h_codes[:].bitcast(FP8X4), scales=h_sc[:], in_=hid[:].rearrange("p r t -> p (r t)"))
-            acc = psum.tile([P, HALF], F32, name="y", bufs=4)
+            acc = psum.tile([P, HALF], F32, name="y", bufs=3)
             nc.tensor.matmul_mx(
                 out=acc[:, :RW],
                 lhsT=w2_codes[:].bitcast(FP8X4),

@@ -19,11 +19,18 @@ AX = mybir.AxisListType
 
 P = 128
 PACK = 4
-HALF = 512
+PER_COLUMN = 16
+QUADRANT = 32
+LINE = 4
+HALF = S // 2
 GROUPS = HALF // D
-WINDOW = U + 16
+UNITS = 2 * PACK
+WINDOW = U + PER_COLUMN
 GUESS_RATE = 0.9625
 GUESS_FLOOR = 0.107
+SUM_LAG = 2
+GAP_LAG = 3
+DIVIDE_LAG = 5
 
 
 def tile_picked_ymaskd_mix_p_kernel(
@@ -32,191 +39,224 @@ def tile_picked_ymaskd_mix_p_kernel(
     nc = tc.nc
     with ExitStack() as ctx:
         keep = ctx.enter_context(tc.tile_pool(name="keep", bufs=1))
-        ring = ctx.enter_context(tc.tile_pool(name="ring", bufs=4))
+        ring = ctx.enter_context(tc.tile_pool(name="ring", bufs=3))
         psum = ctx.enter_context(tc.psum_pool(name="psum", bufs=1))
 
-        offs_sb = keep.tile([P, S // 16], U16, name="offs_sb")
-        slot_sb = keep.tile([P, U // 16], U16, name="slot_sb")
-        xs = keep.tile([P, T], U8, name="xs", align_bytes=64)
-        nc.vector.memset(xs[:].bitcast(I32), 0)
+        offs_sb = keep.tile([P, S // PER_COLUMN], U16, name="offs_sb")
+        slot_sb = keep.tile([P, U // PER_COLUMN], U16, name="slot_sb")
+        scale_table = keep.tile([P, T], U8, name="scale_table", align_bytes=64)
+        nc.vector.memset(scale_table[:].bitcast(I32), 0)
         nc.sync.dma_start(offs_sb[:], offs)
-        xw = keep.tile([P, T], I32, name="xw", align_bytes=64)
-        nc.sync.dma_start(out=xw[:], in_=x_words[0].rearrange("p n t -> p (n t)").bitcast(I32))
-        w1v = w1.rearrange("(p j) c -> p j c", j=PACK)
+        word_table = keep.tile([P, T], I32, name="word_table", align_bytes=64)
+        nc.sync.dma_start(out=word_table[:], in_=x_words[0].rearrange("p n j -> p (n j)").bitcast(I32))
+        for q in range(P // QUADRANT):
+            nc.sync.dma_start(
+                out=scale_table[QUADRANT * q : QUADRANT * q + 4, :].bitcast(I32),
+                in_=x_scales[0, 4 * q : 4 * q + 4, :].bitcast(I32),
+            )
+        w1_rows = w1.rearrange("(p j) c -> p j c", j=PACK)
         w1_raw = []
         for s in range(2):
-            raw = keep.tile([P, PACK, H // 2], F32, name="w1_raw%d" % s, tag="stage%d" % s)
-            nc.sync.dma_start(out=raw[:], in_=w1v[:, :, s * (H // 2) : (s + 1) * (H // 2)])
+            raw = keep.tile([P, PACK, H // 2], F32, name="w1_raw%d" % s)
+            nc.sync.dma_start(out=raw[:], in_=w1_rows[:, :, s * (H // 2) : (s + 1) * (H // 2)])
             w1_raw.append(raw)
-        for q in range(4):
-            nc.scalar.dma_start(
-                out=xs[32 * q : 32 * q + 4, :].bitcast(I32), in_=x_scales[0, 4 * q : 4 * q + 4, :].bitcast(I32)
-            )
         nc.sync.dma_start(slot_sb[:], slot)
         unit_sb = keep.tile([P, PACK], F32, name="unit_sb")
-        nc.gpsimd.dma_start(out=unit_sb[:], in_=unit.rearrange("(p t) o -> p (t o)", t=PACK))
+        nc.sync.dma_start(out=unit_sb[:], in_=unit.rearrange("(p t) o -> p (t o)", t=PACK))
 
         ident = keep.tile([P, P], F32, name="ident")
         make_identity(nc, ident[:])
-        best_win, ev_win = [], []
+        best_win, minus_ev_win = [], []
         for t in range(PACK):
-            bw = keep.tile([P, WINDOW], F32, name="best_win%d" % t)
-            ew = keep.tile([P, WINDOW], F32, name="ev_win%d" % t)
-            nc.gpsimd.memset(bw[:, V:], 0.0)
-            nc.gpsimd.memset(ew[:, V:], 0.0)
-            best_win.append(bw)
-            ev_win.append(ew)
+            best_t = keep.tile([P, WINDOW], F32, name="best_win%d" % t)
+            minus_ev_t = keep.tile([P, WINDOW], F32, name="minus_ev_win%d" % t)
+            nc.gpsimd.memset(best_t[:, V:], 0.0)
+            nc.gpsimd.memset(minus_ev_t[:, V:], 0.0)
+            best_win.append(best_t)
+            minus_ev_win.append(minus_ev_t)
 
         x_codes = [keep.tile([P, HALF], U32, name="x_codes%d" % h, align_bytes=64) for h in range(2)]
-        x_sc = [keep.tile([P, HALF], U8, name="x_sc%d" % h, align_bytes=64) for h in range(2)]
-        parts = [offs_sb[:, h * (HALF // 16) : (h + 1) * (HALF // 16)] for h in range(2)]
-        for h in range(2):
-            nc.vector.tensor_copy(x_codes[h][:], xw[:].bitcast(U32).indirect(parts[h]))
-        nc.vector.tensor_copy(x_sc[0][:], xs[:].indirect(parts[0]))
-
-        w1_bf = keep.tile([P, PACK, P, PACK], BF16, name="w1_bf", tag="stage2", align_bytes=64)
+        x_bytes = [keep.tile([P, HALF], U8, name="x_bytes0", align_bytes=64)]
+        w1_bf = keep.tile([P, PACK, P, PACK], BF16, name="w1_bf", tag="w1_bf", align_bytes=64)
         for s in range(2):
-            dst = w1_bf[:, :, s * 64 : (s + 1) * 64, :].rearrange("p t m j -> p m j t")
-            src = w1_raw[s][:].rearrange("p j (m t) -> p m j t", t=PACK)
-            nc.scalar.activation(dst, src, ACT.Copy)
-        w1_codes = keep.tile([P, PACK, P], U32, name="w1_codes", align_bytes=64)
-        w1_sc = keep.tile([P, PACK, P], U8, name="w1_sc", align_bytes=64)
-        for t in range(PACK):
-            nc.vector.quantize_mx(
-                out=w1_codes[:, t, :].bitcast(FP8X4),
-                scales=w1_sc[:, t, :],
-                in_=w1_bf[:, t, :, :].rearrange("p m j -> p (m j)"),
+            nc.scalar.activation(
+                w1_bf[:, :, s * (P // 2) : (s + 1) * (P // 2), :].rearrange("p t m j -> p m j t"),
+                w1_raw[s][:].rearrange("p j (m t) -> p m j t", t=PACK),
+                ACT.Copy,
             )
-        nc.vector.tensor_copy(x_sc[1][:], xs[:].indirect(parts[1]))
+        w1_codes = keep.tile([P, PACK, P], U32, name="w1_codes", align_bytes=64)
+        w1_bytes = keep.tile([P, PACK, P], U8, name="w1_bytes", align_bytes=64)
+        for t0, t1 in ((0, 1), (1, PACK)):
+            nc.vector.quantize_mx(
+                out=w1_codes[:, t0:t1, :].rearrange("p t m -> p (t m)").bitcast(FP8X4),
+                scales=w1_bytes[:, t0:t1, :].rearrange("p t m -> p (t m)"),
+                in_=w1_bf[:, t0:t1, :, :].rearrange("p t m j -> p (t m j)"),
+            )
+        x_bytes.append(keep.tile([P, HALF], U8, name="x_bytes1", tag="w1_bf", align_bytes=64))
+        for h in range(2):
+            picked = offs_sb[:, h * (HALF // PER_COLUMN) : (h + 1) * (HALF // PER_COLUMN)]
+            nc.vector.tensor_copy(x_bytes[h][:], scale_table[:].indirect(picked))
+            nc.vector.tensor_copy(x_codes[h][:], word_table[:].bitcast(U32).indirect(picked))
 
-        mk_sb = keep.tile([P, PACK, U], F32, name="mk_sb", tag="stage0")
+        mk_sb = keep.tile([P, PACK, U], F32, name="mk_sb")
         nc.sync.dma_start(out=mk_sb[:], in_=mk.rearrange("(p t) r -> p t r", t=PACK))
-        thr_sb = keep.tile([P, PACK, U], F32, name="thr_sb", tag="stage1")
+        w2_raw = keep.tile([P, PACK, N], F32, name="w2_raw")
+        nc.sync.dma_start(out=w2_raw[:], in_=w2.rearrange("(p t) n -> p t n", t=PACK))
+        w2_bf = keep.tile([P, N, PACK], BF16, name="w2_bf", align_bytes=64)
+        nc.gpsimd.tensor_copy(
+            w2_bf[:].rearrange("p (c i) t -> p c t i", i=LINE), w2_raw[:].rearrange("p t (c i) -> p c t i", i=LINE)
+        )
+        thr_sb = keep.tile([P, PACK, U], F32, name="thr_sb")
         nc.sync.dma_start(out=thr_sb[:], in_=thr.rearrange("(p t) r -> p t r", t=PACK))
-        w2_raw = keep.tile([P, PACK, N], F32, name="w2_raw", tag="stage2", align_bytes=64)
-        nc.sync.dma_start(out=w2_raw[:], in_=w2.rearrange("(p j) n -> p j n", j=PACK))
 
         half_unit = keep.tile([P, PACK], F32, name="half_unit")
         nc.gpsimd.tensor_scalar(half_unit[:], unit_sb[:], 0.5, 0.0, ALU.mult, ALU.add)
-        mask_u = keep.tile([P, PACK, U], F32, name="mask_u")
-        mask_hu = keep.tile([P, PACK, U], F32, name="mask_hu")
-        for t in range(PACK):
-            nc.gpsimd.tensor_scalar(mask_hu[:, t, :], mk_sb[:, t, :], unit_sb[:, t : t + 1], 0.5, ALU.mult, ALU.mult)
-        for t in range(PACK):
-            nc.gpsimd.tensor_scalar(mask_u[:, t, :], mk_sb[:, t, :], unit_sb[:, t : t + 1], 0.0, ALU.mult, ALU.add)
-
+        unit_mk = keep.tile([P, PACK, U], F32, name="unit_mk")
+        tanh_sb = keep.tile([P, PACK, U], F32, name="tanh_sb")
         kept = keep.tile([P, PACK, U], F32, name="kept")
         gap = keep.tile([P, PACK, U], F32, name="gap")
+        for t in range(PACK):
+            nc.gpsimd.tensor_scalar(unit_mk[:, t, :], mk_sb[:, t, :], unit_sb[:, t : t + 1], 0.0, ALU.mult, ALU.add)
 
-        def scores(t):
-            ssum = psum.tile([P, V], F32, name="ssum", bufs=2)
-            nsum = psum.tile([P, V], F32, name="nsum", bufs=2)
-            for h in range(2):
-                cols = slice(h * GROUPS, (h + 1) * GROUPS)
-                y = psum.tile([P, HALF], F32, name="y", bufs=3)
-                nc.tensor.matmul_mx(
-                    out=y[:],
-                    lhsT=w1_codes[:, t, :].bitcast(FP8X4),
-                    lhsT_scale=w1_sc[:, t, :],
-                    rhs=x_codes[h][:].bitcast(FP8X4),
-                    rhs_scale=x_sc[h][:],
-                    start=True,
-                    stop=True,
-                )
-                top = best_win[t][:, cols]
-                nc.vector.tensor_reduce(top, y[:].rearrange("p (v d) -> p v d", d=D), AX.X, ALU.max)
-                y_planes = y[:].rearrange("p (v d) -> p d v", d=D)
-                z = ring.tile([P, D, GROUPS], F32, name="z")
-                nc.vector.tensor_tensor(z[:], y_planes, top.unsqueeze(1).to_broadcast([P, D, GROUPS]), ALU.subtract)
-                e = ring.tile([P, D, GROUPS], F32, name="e")
-                nc.scalar.activation(e[:], z[:], ACT.Exp)
-                ey = ring.tile([P, D, GROUPS], F32, name="ey")
-                nc.vector.tensor_tensor(ey[:], y_planes, e[:], ALU.mult)
-                for d in range(D):
-                    nc.tensor.matmul(ssum[:, cols], e[:, d, :], ident[:], start=(d == 0), stop=(d == D - 1), is_transpose=True)
-                for d in range(D):
-                    nc.tensor.matmul(nsum[:, cols], ey[:, d, :], ident[:], start=(d == 0), stop=(d == D - 1), is_transpose=True)
-            return ssum, nsum
+        scores, shifted, exps, sums, turned = {}, {}, {}, {}, {}
 
-        def divide(t, ssum, nsum):
+        def product(u):
+            t, h = divmod(u, 2)
+            y = psum.tile([P, HALF], F32, name="y", bufs=4)
+            nc.tensor.matmul_mx(
+                out=y[:],
+                lhsT=w1_codes[:, t, :].bitcast(FP8X4),
+                lhsT_scale=w1_bytes[:, t, :],
+                rhs=x_codes[h][:].bitcast(FP8X4),
+                rhs_scale=x_bytes[h][:],
+                start=True,
+                stop=True,
+            )
+            scores[u] = y
+
+        def exponentials(u):
+            t, h = divmod(u, 2)
+            y = scores[u]
+            top = best_win[t][:, h * GROUPS : (h + 1) * GROUPS]
+            nc.vector.tensor_reduce(top, y[:].rearrange("p (v d) -> p v d", d=D), AX.X, ALU.max)
+            z = ring.tile([P, D, GROUPS], F32, name="z", tag="z")
+            nc.vector.tensor_tensor(
+                z[:], y[:].rearrange("p (v d) -> p d v", d=D), top.unsqueeze(1).to_broadcast([P, D, GROUPS]), ALU.subtract
+            )
+            e = ring.tile([P, D, GROUPS], F32, name="e")
+            nc.scalar.activation(e[:], z[:], ACT.Exp)
+            shifted[u], exps[u] = z, e
+
+        def add_up(u):
+            t, h = divmod(u, 2)
+            cols = slice(h * GROUPS, (h + 1) * GROUPS)
+            if h == 0:
+                sums[t] = psum.tile([P, 2, V], F32, name="sums", bufs=2)
+            e = exps[u]
+            weighted = ring.tile([P, D, GROUPS], F32, name="weighted")
+            if t == 0:
+                nc.gpsimd.tensor_tensor(weighted[:], shifted[u][:], e[:], ALU.mult)
+            else:
+                nc.vector.tensor_tensor(weighted[:], scores[u][:].rearrange("p (v d) -> p d v", d=D), e[:], ALU.mult)
+            for k, terms in enumerate((e, weighted)):
+                for d in range(D):
+                    nc.tensor.matmul(
+                        sums[t][:, k, cols], terms[:, d, :], ident[:], start=(d == 0), stop=(d == D - 1), is_transpose=True
+                    )
+
+        def start_division(t):
             guess = ring.tile([P, V], F32, name="guess")
-            nc.scalar.activation(guess[:], ssum[:], ACT.Exp, scale=-GUESS_RATE)
-            half_t = ring.tile([P, V], F32, name="half_t")
-            nc.vector.scalar_tensor_tensor(half_t[:], guess[:], GUESS_FLOOR, ssum[:], ALU.add, ALU.mult)
-            eps2 = ring.tile([P, V], F32, name="eps2")
-            nc.scalar.activation(eps2[:], half_t[:], ACT.Square, bias=-1.0, scale=2.0)
+            nc.scalar.activation(guess[:], sums[t][:, 0, :], ACT.Exp, scale=-GUESS_RATE)
+            half_sr = ring.tile([P, V], F32, name="half_sr")
+            nc.vector.scalar_tensor_tensor(half_sr[:], guess[:], GUESS_FLOOR, sums[t][:, 0, :], ALU.add, ALU.mult)
+            half_nr = ring.tile([P, V], F32, name="half_nr")
+            nc.vector.scalar_tensor_tensor(half_nr[:], guess[:], GUESS_FLOOR, sums[t][:, 1, :], ALU.add, ALU.mult)
+            turned[t] = psum.tile([P, 2, V], F32, name="turned", bufs=2)
+            for k, src in enumerate((half_sr, half_nr)):
+                for c0 in range(0, V, GROUPS):
+                    nc.tensor.transpose(turned[t][:, k, c0 : c0 + GROUPS], src[:, c0 : c0 + GROUPS], ident[:])
+
+        def end_division(t):
+            half_sr, half_nr = turned[t][:, 0, :], turned[t][:, 1, :]
+            x2 = ring.tile([P, V], F32, name="x2")
+            nc.scalar.activation(x2[:], half_sr, ACT.Square, bias=-1.0, scale=2.0)
             series = ring.tile([P, V], F32, name="series")
-            nc.scalar.activation(series[:], eps2[:], ACT.Square, bias=0.5)
-            q1 = ring.tile([P, V], F32, name="q1")
-            nc.vector.scalar_tensor_tensor(q1[:], guess[:], GUESS_FLOOR, nsum[:], ALU.add, ALU.mult)
-            q2 = ring.tile([P, V], F32, name="q2")
-            nc.vector.scalar_tensor_tensor(q2[:], half_t[:], 1.0, q1[:], ALU.subtract, ALU.mult)
-            q3 = ring.tile([P, V], F32, name="q3")
-            nc.vector.scalar_tensor_tensor(q3[:], series[:], 0.75, q2[:], ALU.add, ALU.mult)
-            back = psum.tile([P, V], F32, name="back", bufs=1)
-            for h in range(2):
-                cols = slice(h * GROUPS, (h + 1) * GROUPS)
-                nc.tensor.transpose(back[:, cols], q3[:, cols], ident[:])
-            nc.scalar.activation(ev_win[t][:, :V], back[:], ACT.Copy, scale=-4.0)
+            nc.scalar.activation(series[:], x2[:], ACT.Square, bias=1.0, scale=2.0)
+            partial = ring.tile([P, V], F32, name="partial")
+            nc.vector.scalar_tensor_tensor(partial[:], series[:], 3.0, half_nr, ALU.add, ALU.mult)
+            if t == 0:
+                minus_mean_z = ring.tile([P, V], F32, name="minus_mean_z")
+                nc.vector.scalar_tensor_tensor(minus_mean_z[:], half_sr, 1.0, partial[:], ALU.subtract, ALU.mult)
+                nc.vector.tensor_tensor(minus_ev_win[t][:, :V], minus_mean_z[:], best_win[t][:, :V], ALU.subtract)
+            else:
+                nc.vector.scalar_tensor_tensor(minus_ev_win[t][:, :V], half_sr, 1.0, partial[:], ALU.subtract, ALU.mult)
 
         def gaps(t):
             ms = ring.tile([P, U], F32, name="ms")
             nc.scalar.activation(ms[:], best_win[t][:].indirect(slot_sb[:]), ACT.Copy)
-            nc.vector.scalar_tensor_tensor(gap[:, t, :], ms[:], half_unit[:, t : t + 1], mask_hu[:, t, :], ALU.mult, ALU.subtract)
+            ms_less_mk = ring.tile([P, U], F32, name="ms_less_mk", tag="z")
+            nc.gpsimd.tensor_tensor(ms_less_mk[:], ms[:], mk_sb[:, t, :], ALU.subtract)
+            nc.gpsimd.tensor_scalar(gap[:, t, :], ms_less_mk[:], half_unit[:, t : t + 1], 0.0, ALU.mult, ALU.add)
 
-        def keeps(t, r0, r1):
-            cs = ring.tile([P, r1 - r0], F32, name="cs")
-            nc.scalar.activation(cs[:], ev_win[t][:].indirect(slot_sb[:, r0 // 16 : r1 // 16]), ACT.Copy)
-            margin = ring.tile([P, r1 - r0], F32, name="margin")
-            nc.vector.tensor_tensor(margin[:], cs[:], thr_sb[:, t, r0:r1], ALU.subtract)
-            th = ring.tile([P, r1 - r0], F32, name="th")
-            nc.scalar.activation(th[:], margin[:], ACT.Tanh)
-            nc.vector.scalar_tensor_tensor(kept[:, t, r0:r1], th[:], 1.0, gap[:, t, r0:r1], ALU.add, ALU.mult)
+        def keeps(t, r0, r1, gather_on_vector):
+            looked_up = minus_ev_win[t][:].indirect(slot_sb[:, r0 // PER_COLUMN : r1 // PER_COLUMN])
+            if not gather_on_vector:
+                minus_cs = ring.tile([P, r1 - r0], F32, name="minus_cs")
+                nc.scalar.activation(minus_cs[:], looked_up, ACT.Copy)
+                looked_up = minus_cs[:]
+            thr_less_cs = ring.tile([P, r1 - r0], F32, name="thr_less_cs")
+            nc.vector.tensor_tensor(thr_less_cs[:], looked_up, thr_sb[:, t, r0:r1], ALU.add)
+            nc.scalar.activation(tanh_sb[:, t, r0:r1], thr_less_cs[:], ACT.Tanh, scale=-1.0)
+            nc.vector.scalar_tensor_tensor(
+                kept[:, t, r0:r1], tanh_sb[:, t, r0:r1], 1.0, gap[:, t, r0:r1], ALU.add, ALU.mult
+            )
 
-        sums = []
-        for t in range(PACK):
-            sums.append(scores(t))
-            if t > 0:
-                divide(t - 1, *sums[t - 1])
-        divide(PACK - 1, *sums[PACK - 1])
-        for t in range(PACK):
-            gaps(t)
-            if t < PACK - 1:
-                keeps(t, 0, U)
-        for g in range(2):
-            keeps(PACK - 1, g * (U // 2), (g + 1) * (U // 2))
+        def all_keeps(t):
+            keeps(t, 0, U, gather_on_vector=False)
 
-        w2_bf = keep.tile([P, N, PACK], BF16, name="w2_bf", align_bytes=64)
-        nc.scalar.activation(
-            w2_bf[:].rearrange("p (c i) j -> p c j i", i=4), w2_raw[:].rearrange("p j (c i) -> p c j i", i=4), ACT.Copy
-        )
+        for u in range(UNITS):
+            product(u)
+        for step in range(UNITS + DIVIDE_LAG + 1):
+            if step < UNITS:
+                exponentials(step)
+            if step - GAP_LAG in range(1, UNITS, 2):
+                gaps((step - GAP_LAG) // 2)
+            if step - SUM_LAG in range(UNITS):
+                add_up(step - SUM_LAG)
+            for stage, lag in ((start_division, DIVIDE_LAG), (end_division, DIVIDE_LAG + 1), (all_keeps, DIVIDE_LAG + 2)):
+                if step - lag in range(1, UNITS, 2):
+                    stage((step - lag) // 2)
+
         w2_codes = keep.tile([P, N], U32, name="w2_codes", align_bytes=64)
-        w2_sc = keep.tile([P, N], U8, name="w2_sc", align_bytes=64)
-        nc.vector.quantize_mx(out=w2_codes[:].bitcast(FP8X4), scales=w2_sc[:], in_=w2_bf[:].rearrange("p n j -> p (n j)"))
+        w2_bytes = keep.tile([P, N], U8, name="w2_bytes", align_bytes=64)
+        nc.vector.quantize_mx(out=w2_codes[:].bitcast(FP8X4), scales=w2_bytes[:], in_=w2_bf[:].rearrange("p n t -> p (n t)"))
 
-        RW = U // 2
+        width = U // 2
         for g in range(2):
-            cols = slice(g * RW, (g + 1) * RW)
-            hid = keep.tile([P, RW, PACK], BF16, name="hid%d" % g, align_bytes=64)
+            cols = slice(g * width, (g + 1) * width)
+            keeps(PACK - 1, cols.start, cols.stop, gather_on_vector=(g == 0))
+            hid = keep.tile([P, width, PACK], BF16, name="hid%d" % g, align_bytes=64)
             nc.vector.tensor_tensor(
-                hid[:].rearrange("p (c i) t -> p c t i", i=4),
-                kept[:, :, cols].rearrange("p t (c i) -> p c t i", i=4),
-                mask_u[:, :, cols].rearrange("p t (c i) -> p c t i", i=4),
+                hid[:].rearrange("p (c i) t -> p c t i", i=LINE),
+                kept[:, :, cols].rearrange("p t (c i) -> p c t i", i=LINE),
+                unit_mk[:, :, cols].rearrange("p t (c i) -> p c t i", i=LINE),
                 ALU.add,
             )
-            h_codes = keep.tile([P, RW], U32, name="h_codes%d" % g, align_bytes=64)
-            h_sc = keep.tile([P, RW], U8, name="h_sc%d" % g, align_bytes=64)
-            nc.vector.quantize_mx(out=h_codes[:].bitcast(FP8X4), scales=h_sc[:], in_=hid[:].rearrange("p r t -> p (r t)"))
-            acc = psum.tile([P, HALF], F32, name="y", bufs=3)
+            hid_codes = keep.tile([P, width], U32, name="hid_codes%d" % g, align_bytes=64)
+            hid_bytes = keep.tile([P, width], U8, name="hid_bytes%d" % g, align_bytes=64)
+            nc.vector.quantize_mx(
+                out=hid_codes[:].bitcast(FP8X4), scales=hid_bytes[:], in_=hid[:].rearrange("p r t -> p (r t)")
+            )
+            acc = psum.tile([P, HALF], F32, name="y", bufs=4)
             nc.tensor.matmul_mx(
-                out=acc[:, :RW],
+                out=acc[:, :width],
                 lhsT=w2_codes[:].bitcast(FP8X4),
-                lhsT_scale=w2_sc[:],
-                rhs=h_codes[:].bitcast(FP8X4),
-                rhs_scale=h_sc[:],
+                lhsT_scale=w2_bytes[:],
+                rhs=hid_codes[:].bitcast(FP8X4),
+                rhs_scale=hid_bytes[:],
                 start=True,
                 stop=True,
             )
-            res = keep.tile([P, RW], F32, name="res%d" % g)
-            nc.scalar.activation(res[:], acc[:, :RW], ACT.Copy)
-            nc.sync.dma_start(out=out[:, cols], in_=res[:])
+            result = keep.tile([P, width], F32, name="result%d" % g)
+            nc.scalar.activation(result[:], acc[:, :width], ACT.Copy)
+            nc.sync.dma_start(out=out[:, cols], in_=result[:])

@@ -39,7 +39,7 @@ def tile_picked_ymaskd_mix_p_kernel(
     nc = tc.nc
     with ExitStack() as ctx:
         keep = ctx.enter_context(tc.tile_pool(name="keep", bufs=1))
-        ring = ctx.enter_context(tc.tile_pool(name="ring", bufs=3))
+        ring = ctx.enter_context(tc.tile_pool(name="ring", bufs=4))
         psum = ctx.enter_context(tc.psum_pool(name="psum", bufs=1))
 
         offs_sb = keep.tile([P, S // PER_COLUMN], U16, name="offs_sb")
@@ -54,12 +54,8 @@ def tile_picked_ymaskd_mix_p_kernel(
                 out=scale_table[QUADRANT * q : QUADRANT * q + 4, :].bitcast(I32),
                 in_=x_scales[0, 4 * q : 4 * q + 4, :].bitcast(I32),
             )
-        w1_rows = w1.rearrange("(p j) c -> p j c", j=PACK)
-        w1_raw = []
-        for s in range(2):
-            raw = keep.tile([P, PACK, H // 2], F32, name="w1_raw%d" % s)
-            nc.sync.dma_start(out=raw[:], in_=w1_rows[:, :, s * (H // 2) : (s + 1) * (H // 2)])
-            w1_raw.append(raw)
+        w1_raw = keep.tile([P, PACK, H], F32, name="w1_raw")
+        nc.sync.dma_start(out=w1_raw[:], in_=w1.rearrange("(p j) c -> p j c", j=PACK))
         nc.sync.dma_start(slot_sb[:], slot)
         unit_sb = keep.tile([P, PACK], F32, name="unit_sb")
         nc.sync.dma_start(out=unit_sb[:], in_=unit.rearrange("(p t) o -> p (t o)", t=PACK))
@@ -77,22 +73,21 @@ def tile_picked_ymaskd_mix_p_kernel(
 
         x_codes = [keep.tile([P, HALF], U32, name="x_codes%d" % h, align_bytes=64) for h in range(2)]
         x_bytes = [keep.tile([P, HALF], U8, name="x_bytes0", align_bytes=64)]
-        w1_bf = keep.tile([P, PACK, P, PACK], BF16, name="w1_bf", tag="w1_bf", align_bytes=64)
-        for s in range(2):
-            nc.scalar.activation(
-                w1_bf[:, :, s * (P // 2) : (s + 1) * (P // 2), :].rearrange("p t m j -> p m j t"),
-                w1_raw[s][:].rearrange("p j (m t) -> p m j t", t=PACK),
-                ACT.Copy,
-            )
         w1_codes = keep.tile([P, PACK, P], U32, name="w1_codes", align_bytes=64)
         w1_bytes = keep.tile([P, PACK, P], U8, name="w1_bytes", align_bytes=64)
-        for t0, t1 in ((0, 1), (1, PACK)):
-            nc.vector.quantize_mx(
-                out=w1_codes[:, t0:t1, :].rearrange("p t m -> p (t m)").bitcast(FP8X4),
-                scales=w1_bytes[:, t0:t1, :].rearrange("p t m -> p (t m)"),
-                in_=w1_bf[:, t0:t1, :, :].rearrange("p t m j -> p (t m j)"),
+        for t0 in range(0, PACK, 2):
+            w1_bf = keep.tile([P, 2, P, PACK], BF16, name="w1_bf%d" % t0, tag="w1_bf%d" % t0, align_bytes=64)
+            nc.scalar.activation(
+                w1_bf[:].rearrange("p t m j -> p m j t"),
+                w1_raw[:].rearrange("p j (m t) -> p m j t", t=PACK)[:, :, :, t0 : t0 + 2],
+                ACT.Copy,
             )
-        x_bytes.append(keep.tile([P, HALF], U8, name="x_bytes1", tag="w1_bf", align_bytes=64))
+            nc.vector.quantize_mx(
+                out=w1_codes[:, t0 : t0 + 2, :].rearrange("p t m -> p (t m)").bitcast(FP8X4),
+                scales=w1_bytes[:, t0 : t0 + 2, :].rearrange("p t m -> p (t m)"),
+                in_=w1_bf[:].rearrange("p t m j -> p (t m j)"),
+            )
+        x_bytes.append(keep.tile([P, HALF], U8, name="x_bytes1", tag="w1_bf0", align_bytes=64))
         for h in range(2):
             picked = offs_sb[:, h * (HALF // PER_COLUMN) : (h + 1) * (HALF // PER_COLUMN)]
             nc.vector.tensor_copy(x_bytes[h][:], scale_table[:].indirect(picked))
@@ -103,15 +98,15 @@ def tile_picked_ymaskd_mix_p_kernel(
         w2_raw = keep.tile([P, PACK, N], F32, name="w2_raw")
         nc.sync.dma_start(out=w2_raw[:], in_=w2.rearrange("(p t) n -> p t n", t=PACK))
         w2_bf = keep.tile([P, N, PACK], BF16, name="w2_bf", align_bytes=64)
-        nc.gpsimd.tensor_copy(
-            w2_bf[:].rearrange("p (c i) t -> p c t i", i=LINE), w2_raw[:].rearrange("p t (c i) -> p c t i", i=LINE)
+        nc.scalar.activation(
+            w2_bf[:].rearrange("p (c i) t -> p c t i", i=LINE),
+            w2_raw[:].rearrange("p t (c i) -> p c t i", i=LINE),
+            ACT.Copy,
         )
         thr_sb = keep.tile([P, PACK, U], F32, name="thr_sb")
         nc.sync.dma_start(out=thr_sb[:], in_=thr.rearrange("(p t) r -> p t r", t=PACK))
 
-        half_unit = keep.tile([P, PACK], F32, name="half_unit")
-        nc.gpsimd.tensor_scalar(half_unit[:], unit_sb[:], 0.5, 0.0, ALU.mult, ALU.add)
-        unit_mk = keep.tile([P, PACK, U], F32, name="unit_mk")
+        unit_mk = keep.tile([P, PACK, U], F32, name="unit_mk", tag="w1_bf2", align_bytes=64)
         tanh_sb = keep.tile([P, PACK, U], F32, name="tanh_sb")
         kept = keep.tile([P, PACK, U], F32, name="kept")
         gap = keep.tile([P, PACK, U], F32, name="gap")
@@ -196,7 +191,7 @@ def tile_picked_ymaskd_mix_p_kernel(
             nc.scalar.activation(ms[:], best_win[t][:].indirect(slot_sb[:]), ACT.Copy)
             ms_less_mk = ring.tile([P, U], F32, name="ms_less_mk", tag="z")
             nc.gpsimd.tensor_tensor(ms_less_mk[:], ms[:], mk_sb[:, t, :], ALU.subtract)
-            nc.gpsimd.tensor_scalar(gap[:, t, :], ms_less_mk[:], half_unit[:, t : t + 1], 0.0, ALU.mult, ALU.add)
+            nc.gpsimd.tensor_scalar(gap[:, t, :], ms_less_mk[:], unit_sb[:, t : t + 1], 0.5, ALU.mult, ALU.mult)
 
         def keeps(t, r0, r1, gather_on_vector):
             looked_up = minus_ev_win[t][:].indirect(slot_sb[:, r0 // PER_COLUMN : r1 // PER_COLUMN])
@@ -211,9 +206,6 @@ def tile_picked_ymaskd_mix_p_kernel(
                 kept[:, t, r0:r1], tanh_sb[:, t, r0:r1], 1.0, gap[:, t, r0:r1], ALU.add, ALU.mult
             )
 
-        def all_keeps(t):
-            keeps(t, 0, U, gather_on_vector=False)
-
         for u in range(UNITS):
             product(u)
         for step in range(UNITS + DIVIDE_LAG + 1):
@@ -223,9 +215,12 @@ def tile_picked_ymaskd_mix_p_kernel(
                 gaps((step - GAP_LAG) // 2)
             if step - SUM_LAG in range(UNITS):
                 add_up(step - SUM_LAG)
-            for stage, lag in ((start_division, DIVIDE_LAG), (end_division, DIVIDE_LAG + 1), (all_keeps, DIVIDE_LAG + 2)):
+            for stage, lag in ((start_division, DIVIDE_LAG), (end_division, DIVIDE_LAG + 1)):
                 if step - lag in range(1, UNITS, 2):
                     stage((step - lag) // 2)
+
+        for t in range(PACK - 1):
+            keeps(t, 0, U, gather_on_vector=False)
 
         w2_codes = keep.tile([P, N], U32, name="w2_codes", align_bytes=64)
         w2_bytes = keep.tile([P, N], U8, name="w2_bytes", align_bytes=64)

from contextlib import ExitStack

import concourse.mybir as mybir
from concourse.masks import make_identity

K, T, S, D, N, H, V, U = 512, 2048, 1024, 4, 128, 512, 256, 512
FLOPS = 2 * K * H * S + 2 * H * N * U

F32 = mybir.dt.float32
BF16 = mybir.dt.bfloat16
I32 = mybir.dt.int32
U32 = mybir.dt.uint32
U16 = mybir.dt.uint16
U8 = mybir.dt.uint8
FP8X4 = mybir.dt.float8_e4m3fn_x4
ALU = mybir.AluOpType
ACT = mybir.ActivationFunctionType
AX = mybir.AxisListType

P = 128
PACK = 4
PER_COLUMN = 16
QUADRANT = 32
LINE = 4
HALF = S // 2
GROUPS = HALF // D
UNITS = 2 * PACK
WINDOW = U + PER_COLUMN
GUESS_RATE = 0.9625
GUESS_FLOOR = 0.107
SUM_LAG = 2
GAP_LAG = 3
DIVIDE_LAG = 5


def tile_picked_ymaskd_mix_p_kernel(
    tc, x_words, x_scales, w1, thr, mk, unit, w2, offs, slot, out
):
    nc = tc.nc
    with ExitStack() as ctx:
        keep = ctx.enter_context(tc.tile_pool(name="keep", bufs=1))
        ring = ctx.enter_context(tc.tile_pool(name="ring", bufs=4))
        psum = ctx.enter_context(tc.psum_pool(name="psum", bufs=1))

        offs_sb = keep.tile([P, S // PER_COLUMN], U16, name="offs_sb")
        slot_sb = keep.tile([P, U // PER_COLUMN], U16, name="slot_sb")
        scale_table = keep.tile([P, T], U8, name="scale_table", align_bytes=64)
        nc.vector.memset(scale_table[:].bitcast(I32), 0)
        nc.sync.dma_start(offs_sb[:], offs)
        word_table = keep.tile([P, T], I32, name="word_table", align_bytes=64)
        nc.sync.dma_start(out=word_table[:], in_=x_words[0].rearrange("p n j -> p (n j)").bitcast(I32))
        for q in range(P // QUADRANT):
            nc.sync.dma_start(
                out=scale_table[QUADRANT * q : QUADRANT * q + 4, :].bitcast(I32),
                in_=x_scales[0, 4 * q : 4 * q + 4, :].bitcast(I32),
            )
        w1_raw = keep.tile([P, PACK, H], F32, name="w1_raw")
        nc.sync.dma_start(out=w1_raw[:], in_=w1.rearrange("(p j) c -> p j c", j=PACK))
        nc.sync.dma_start(slot_sb[:], slot)
        unit_sb = keep.tile([P, PACK], F32, name="unit_sb")
        nc.sync.dma_start(out=unit_sb[:], in_=unit.rearrange("(p t) o -> p (t o)", t=PACK))

        ident = keep.tile([P, P], F32, name="ident")
        make_identity(nc, ident[:])
        best_win, minus_ev_win = [], []
        for t in range(PACK):
            best_t = keep.tile([P, WINDOW], F32, name="best_win%d" % t)
            minus_ev_t = keep.tile([P, WINDOW], F32, name="minus_ev_win%d" % t)
            nc.gpsimd.memset(best_t[:, V:], 0.0)
            nc.gpsimd.memset(minus_ev_t[:, V:], 0.0)
            best_win.append(best_t)
            minus_ev_win.append(minus_ev_t)

        x_codes = [keep.tile([P, HALF], U32, name="x_codes%d" % h, align_bytes=64) for h in range(2)]
        x_bytes = [keep.tile([P, HALF], U8, name="x_bytes0", align_bytes=64)]
        w1_codes = keep.tile([P, PACK, P], U32, name="w1_codes", align_bytes=64)
        w1_bytes = keep.tile([P, PACK, P], U8, name="w1_bytes", align_bytes=64)
        for t0 in range(0, PACK, 2):
            w1_bf = keep.tile([P, 2, P, PACK], BF16, name="w1_bf%d" % t0, tag="w1_bf%d" % t0, align_bytes=64)
            nc.scalar.activation(
                w1_bf[:].rearrange("p t m j -> p m j t"),
                w1_raw[:].rearrange("p j (m t) -> p m j t", t=PACK)[:, :, :, t0 : t0 + 2],
                ACT.Copy,
            )
            nc.vector.quantize_mx(
                out=w1_codes[:, t0 : t0 + 2, :].rearrange("p t m -> p (t m)").bitcast(FP8X4),
                scales=w1_bytes[:, t0 : t0 + 2, :].rearrange("p t m -> p (t m)"),
                in_=w1_bf[:].rearrange("p t m j -> p (t m j)"),
            )
        x_bytes.append(keep.tile([P, HALF], U8, name="x_bytes1", tag="w1_bf0", align_bytes=64))
        for h in range(2):
            picked = offs_sb[:, h * (HALF // PER_COLUMN) : (h + 1) * (HALF // PER_COLUMN)]
            nc.vector.tensor_copy(x_bytes[h][:], scale_table[:].indirect(picked))
            nc.vector.tensor_copy(x_codes[h][:], word_table[:].bitcast(U32).indirect(picked))

        mk_sb = keep.tile([P, PACK, U], F32, name="mk_sb")
        nc.sync.dma_start(out=mk_sb[:], in_=mk.rearrange("(p t) r -> p t r", t=PACK))
        w2_raw = keep.tile([P, PACK, N], F32, name="w2_raw")
        nc.sync.dma_start(out=w2_raw[:], in_=w2.rearrange("(p t) n -> p t n", t=PACK))
        w2_bf = keep.tile([P, N, PACK], BF16, name="w2_bf", align_bytes=64)
        nc.scalar.activation(
            w2_bf[:].rearrange("p (c i) t -> p c t i", i=LINE),
            w2_raw[:].rearrange("p t (c i) -> p c t i", i=LINE),
            ACT.Copy,
        )
        thr_sb = keep.tile([P, PACK, U], F32, name="thr_sb")
        nc.sync.dma_start(out=thr_sb[:], in_=thr.rearrange("(p t) r -> p t r", t=PACK))

        unit_mk = keep.tile([P, PACK, U], F32, name="unit_mk", tag="w1_bf2", align_bytes=64)
        tanh_sb = keep.tile([P, PACK, U], F32, name="tanh_sb")
        kept = keep.tile([P, PACK, U], F32, name="kept")
        gap = keep.tile([P, PACK, U], F32, name="gap")
        for t in range(PACK):
            nc.gpsimd.tensor_scalar(unit_mk[:, t, :], mk_sb[:, t, :], unit_sb[:, t : t + 1], 0.0, ALU.mult, ALU.add)

        scores, shifted, exps, sums, turned = {}, {}, {}, {}, {}

        def product(u):
            t, h = divmod(u, 2)
            y = psum.tile([P, HALF], F32, name="y", bufs=4)
            nc.tensor.matmul_mx(
                out=y[:],
                lhsT=w1_codes[:, t, :].bitcast(FP8X4),
                lhsT_scale=w1_bytes[:, t, :],
                rhs=x_codes[h][:].bitcast(FP8X4),
                rhs_scale=x_bytes[h][:],
                start=True,
                stop=True,
            )
            scores[u] = y

        def exponentials(u):
            t, h = divmod(u, 2)
            y = scores[u]
            top = best_win[t][:, h * GROUPS : (h + 1) * GROUPS]
            nc.vector.tensor_reduce(top, y[:].rearrange("p (v d) -> p v d", d=D), AX.X, ALU.max)
            z = ring.tile([P, D, GROUPS], F32, name="z", tag="z")
            nc.vector.tensor_tensor(
                z[:], y[:].rearrange("p (v d) -> p d v", d=D), top.unsqueeze(1).to_broadcast([P, D, GROUPS]), ALU.subtract
            )
            e = ring.tile([P, D, GROUPS], F32, name="e")
            nc.scalar.activation(e[:], z[:], ACT.Exp)
            shifted[u], exps[u] = z, e

        def add_up(u):
            t, h = divmod(u, 2)
            cols = slice(h * GROUPS, (h + 1) * GROUPS)
            if h == 0:
                sums[t] = psum.tile([P, 2, V], F32, name="sums", bufs=2)
            e = exps[u]
            weighted = ring.tile([P, D, GROUPS], F32, name="weighted")
            if t == 0:
                nc.gpsimd.tensor_tensor(weighted[:], shifted[u][:], e[:], ALU.mult)
            else:
                nc.vector.tensor_tensor(weighted[:], scores[u][:].rearrange("p (v d) -> p d v", d=D), e[:], ALU.mult)
            for k, terms in enumerate((e, weighted)):
                for d in range(D):
                    nc.tensor.matmul(
                        sums[t][:, k, cols], terms[:, d, :], ident[:], start=(d == 0), stop=(d == D - 1), is_transpose=True
                    )

        def start_division(t):
            guess = ring.tile([P, V], F32, name="guess")
            nc.scalar.activation(guess[:], sums[t][:, 0, :], ACT.Exp, scale=-GUESS_RATE)
            half_sr = ring.tile([P, V], F32, name="half_sr")
            nc.vector.scalar_tensor_tensor(half_sr[:], guess[:], GUESS_FLOOR, sums[t][:, 0, :], ALU.add, ALU.mult)
            half_nr = ring.tile([P, V], F32, name="half_nr")
            nc.vector.scalar_tensor_tensor(half_nr[:], guess[:], GUESS_FLOOR, sums[t][:, 1, :], ALU.add, ALU.mult)
            turned[t] = psum.tile([P, 2, V], F32, name="turned", bufs=2)
            for k, src in enumerate((half_sr, half_nr)):
                for c0 in range(0, V, GROUPS):
                    nc.tensor.transpose(turned[t][:, k, c0 : c0 + GROUPS], src[:, c0 : c0 + GROUPS], ident[:])

        def end_division(t):
            half_sr, half_nr = turned[t][:, 0, :], turned[t][:, 1, :]
            x2 = ring.tile([P, V], F32, name="x2")
            nc.scalar.activation(x2[:], half_sr, ACT.Square, bias=-1.0, scale=2.0)
            series = ring.tile([P, V], F32, name="series")
            nc.scalar.activation(series[:], x2[:], ACT.Square, bias=1.0, scale=2.0)
            partial = ring.tile([P, V], F32, name="partial")
            nc.vector.scalar_tensor_tensor(partial[:], series[:], 3.0, half_nr, ALU.add, ALU.mult)
            if t == 0:
                minus_mean_z = ring.tile([P, V], F32, name="minus_mean_z")
                nc.vector.scalar_tensor_tensor(minus_mean_z[:], half_sr, 1.0, partial[:], ALU.subtract, ALU.mult)
                nc.vector.tensor_tensor(minus_ev_win[t][:, :V], minus_mean_z[:], best_win[t][:, :V], ALU.subtract)
            else:
                nc.vector.scalar_tensor_tensor(minus_ev_win[t][:, :V], half_sr, 1.0, partial[:], ALU.subtract, ALU.mult)

        def gaps(t):
            ms = ring.tile([P, U], F32, name="ms")
            nc.scalar.activation(ms[:], best_win[t][:].indirect(slot_sb[:]), ACT.Copy)
            ms_less_mk = ring.tile([P, U], F32, name="ms_less_mk", tag="z")
            nc.gpsimd.tensor_tensor(ms_less_mk[:], ms[:], mk_sb[:, t, :], ALU.subtract)
            nc.gpsimd.tensor_scalar(gap[:, t, :], ms_less_mk[:], unit_sb[:, t : t + 1], 0.5, ALU.mult, ALU.mult)

        def keeps(t, r0, r1, gather_on_vector):
            looked_up = minus_ev_win[t][:].indirect(slot_sb[:, r0 // PER_COLUMN : r1 // PER_COLUMN])
            if not gather_on_vector:
                minus_cs = ring.tile([P, r1 - r0], F32, name="minus_cs")
                nc.scalar.activation(minus_cs[:], looked_up, ACT.Copy)
                looked_up = minus_cs[:]
            thr_less_cs = ring.tile([P, r1 - r0], F32, name="thr_less_cs")
            nc.vector.tensor_tensor(thr_less_cs[:], looked_up, thr_sb[:, t, r0:r1], ALU.add)
            nc.scalar.activation(tanh_sb[:, t, r0:r1], thr_less_cs[:], ACT.Tanh, scale=-1.0)
            nc.vector.scalar_tensor_tensor(
                kept[:, t, r0:r1], tanh_sb[:, t, r0:r1], 1.0, gap[:, t, r0:r1], ALU.add, ALU.mult
            )

        for u in range(UNITS):
            product(u)
        for step in range(UNITS + DIVIDE_LAG + 1):
            if step < UNITS:
                exponentials(step)
            if step - GAP_LAG in range(1, UNITS, 2):
                gaps((step - GAP_LAG) // 2)
            if step - SUM_LAG in range(UNITS):
                add_up(step - SUM_LAG)
            for stage, lag in ((start_division, DIVIDE_LAG), (end_division, DIVIDE_LAG + 1)):
                if step - lag in range(1, UNITS, 2):
                    stage((step - lag) // 2)

        for t in range(PACK - 1):
            keeps(t, 0, U, gather_on_vector=False)

        w2_codes = keep.tile([P, N], U32, name="w2_codes", align_bytes=64)
        w2_bytes = keep.tile([P, N], U8, name="w2_bytes", align_bytes=64)
        nc.vector.quantize_mx(out=w2_codes[:].bitcast(FP8X4), scales=w2_bytes[:], in_=w2_bf[:].rearrange("p n t -> p (n t)"))

        width = U // 2
        for g in range(2):
            cols = slice(g * width, (g + 1) * width)
            keeps(PACK - 1, cols.start, cols.stop, gather_on_vector=(g == 0))
            hid = keep.tile([P, width, PACK], BF16, name="hid%d" % g, align_bytes=64)
            nc.vector.tensor_tensor(
                hid[:].rearrange("p (c i) t -> p c t i", i=LINE),
                kept[:, :, cols].rearrange("p t (c i) -> p c t i", i=LINE),
                unit_mk[:, :, cols].rearrange("p t (c i) -> p c t i", i=LINE),
                ALU.add,
            )
            hid_codes = keep.tile([P, width], U32, name="hid_codes%d" % g, align_bytes=64)
            hid_bytes = keep.tile([P, width], U8, name="hid_bytes%d" % g, align_bytes=64)
            nc.vector.quantize_mx(
                out=hid_codes[:].bitcast(FP8X4), scales=hid_bytes[:], in_=hid[:].rearrange("p r t -> p (r t)")
            )
            acc = psum.tile([P, HALF], F32, name="y", bufs=4)
            nc.tensor.matmul_mx(
                out=acc[:, :width],
                lhsT=w2_codes[:].bitcast(FP8X4),
                lhsT_scale=w2_bytes[:],
                rhs=hid_codes[:].bitcast(FP8X4),
                rhs_scale=hid_bytes[:],
                start=True,
                stop=True,
            )
            result = keep.tile([P, width], F32, name="result%d" % g)
            nc.scalar.activation(result[:], acc[:, :width], ACT.Copy)
            nc.sync.dma_start(out=out[:, cols], in_=result[:])
